import numpy as np
import ml_dtypes


def mxq(x, axis, fmt="e4m3"):
    dtype, down = {"e4m3": (ml_dtypes.float8_e4m3fn, 7), "e5m2": (ml_dtypes.float8_e5m2, 14)}[fmt]
    v = np.moveaxis(np.asarray(x, np.float32).astype(ml_dtypes.bfloat16).astype(np.float64), axis, -1)
    blocks = v.reshape(v.shape[:-1] + (-1, 32))
    amax = np.abs(blocks).max(-1, keepdims=True)
    byte = np.maximum(np.where(amax > 0, np.frexp(amax)[1] - 1 + 127, 0) - down, 1)
    scale = np.exp2(byte - 127.0)
    codes = (blocks / scale).astype(np.float32).astype(dtype).astype(np.float64)
    return np.moveaxis((codes * scale).reshape(v.shape), -1, axis)


WIDE = False


def mx_kscale(k):
    if not WIDE:
        return np.ones(k)
    levels = np.array([10, -10, 5, -5, 0])
    if k % 512:
        return np.exp2(np.random.permutation(np.resize(levels, k // 32))).repeat(32)
    a = np.empty((k // 512, 16))
    for p in range(k // 512):
        a[p, :8] = np.random.permutation(np.resize(levels, 8))
        for g in range(8):
            far = levels[np.abs(levels - a[p, g]) >= 10]
            a[p, g + 8] = far[np.random.randint(len(far))]
    return np.exp2(a.ravel()).repeat(32)


BF16 = ml_dtypes.bfloat16


def bf(x):
    return np.asarray(x, np.float32).astype(BF16)


def f64(x):
    return np.asarray(x).astype(np.float64)

def planes(Y):
    n, m = Y.shape
    b = f64(bf(Y)).reshape(n // 32, 32, m)
    amax = np.abs(b).max(1)
    byte = np.clip(np.where(amax > 0, np.frexp(amax)[1] - 1 + 127 - 7, 1), 1, 254)
    codes = (b * np.exp2(127.0 - byte)[:, None, :]).reshape(n, m).astype(np.float32).astype(ml_dtypes.float8_e4m3fn).view(np.uint8)
    words = codes.reshape(n // 512, 128, 4, m).transpose(0, 1, 3, 2)
    return np.ascontiguousarray(words), np.ascontiguousarray(byte.astype(np.uint8).reshape(n // 512, 16, m))


V, N = 4, 512
EPS = 1e-6


def mean_of_other_views(p):
    views = p.shape[0]
    total = np.sum(p, axis=0, keepdims=True)
    return (total - p) / (views - 1)


def scale_rows(q):
    d = np.mean(np.abs(q), axis=-1)
    return q / (d[:, :, None] + EPS)


def setup_inputs():
    a = mx_kscale(N)
    s = np.random.standard_normal((V, N, N)) / N
    p = np.random.standard_normal((V, N, N)) * 0.01
    return {"s": bf(s * a[None, None, :]), "p": bf(p / a[None, :, None] / a[None, None, :])}


def core(s, p):
    m = mean_of_other_views(f64(p))
    sq = mxq(f64(s), 2, "e4m3")
    t = sq @ mxq(m, 1, "e4m3")
    q = mxq(t, 2, "e4m3") @ sq.transpose(0, 2, 1)
    r = scale_rows(q)
    return 0.5 * (r + np.swapaxes(r, 1, 2))


def reference(s, p):
    R_out = core(s, p)
    words, scales = planes(np.moveaxis(R_out, 1, 0).reshape(512, -1))
    return R_out, words, scales

@@ -1,0 +1,373 @@
+from contextlib import ExitStack
+
+import concourse.mybir as mybir
+from concourse.masks import make_identity
+
+V, N = 4, 512
+P = 128
+J = 4
+FLOPS = 2 * V * 2 * N * N * N
+BYTES = 2 * V * N * N * 2 + V * N * N * 4 + P * V * N * 4 + 16 * V * N
+
+F32 = mybir.dt.float32
+BF16 = mybir.dt.bfloat16
+U32 = mybir.dt.uint32
+I32 = mybir.dt.int32
+U8 = mybir.dt.uint8
+FP8X4 = mybir.dt.float8_e4m3fn_x4
+ADD = mybir.AluOpType.add
+SUB = mybir.AluOpType.subtract
+MULT = mybir.AluOpType.mult
+COPY = mybir.ActivationFunctionType.Copy
+ABS = mybir.ActivationFunctionType.Abs
+
+THIRD = 1.0 / 3.0
+MANUAL = True
+X_ENGINE = "v"
+
+
+def tile_signedsimilaritynetworkcrossdiffusion_x1_kernel(tc, s, p, out_0, out_1, out_2):
+    nc = tc.nc
+    words = out_1[0].rearrange("p m t -> p (m t)").bitcast(I32)
+    scale_rows = out_2[0].bitcast(I32)
+
+    with ExitStack() as ctx:
+        keep = ctx.enter_context(tc.tile_pool(name="keep", bufs=1))
+        work = ctx.enter_context(tc.tile_pool(name="work", bufs=2))
+        psum = ctx.enter_context(tc.psum_pool(name="psum", bufs=8))
+        if MANUAL:
+            ctx.enter_context(tc.manual_schedule())
+
+        def bank(shape, name):
+            return psum.tile(shape, F32, name=name, tag="bank")
+
+        def sbuf(pool, shape, dt, name, bufs):
+            return pool.tile(shape, dt, name=name, tag=name, bufs=bufs, align_bytes=64)
+
+        s_sb, p_sb = [None] * V, [None] * V
+
+        def load_s(v, pieces):
+            s_sb[v] = sbuf(keep, [P, J, N], BF16, "s_sb" + str(v), 1)
+            src = s[v].rearrange("(p t) k -> p t k", t=J)
+            step = J // pieces
+            for t in range(0, J, step):
+                nc.sync.dma_start(out=s_sb[v][:, t : t + step, :], in_=src[:, t : t + step, :])
+
+        def load_p(v):
+            p_sb[v] = sbuf(keep, [P, J, N], BF16, "p_sb" + str(v), 1)
+            nc.sync.dma_start(out=p_sb[v][:], in_=p[v].rearrange("(p t) j -> p t j", t=J))
+
+        load_s(0, 2)
+        for v in (1, 2, 3, 0):
+            load_p(v)
+        for v in range(1, V):
+            load_s(v, 1)
+
+        ident = sbuf(keep, [P, P], F32, "ident", 1)
+        make_identity(nc, ident[:])
+        ident_bf = sbuf(keep, [P, P], BF16, "ident_bf", 1)
+        make_identity(nc, ident_bf[:])
+
+        xt = {}
+        s_codes, s_scales = {}, {}
+        sT = {}
+
+        def XT(v):
+            w = s_sb[v][:].bitcast(F32)
+            for h in range(2):
+                b = bank([P, 2, 2, P], "xt")
+                for tt in range(2):
+                    for u in range(2):
+                        nc.tensor.transpose(b[:, tt, u, :], w[:, 2 * h + tt, u::2], ident[:])
+                xt[v, h] = b
+
+        def XC(v, h, eng):
+            if h == 0:
+                sT[v] = sbuf(work, [P, N, J], BF16, "sT", 2)
+            o = sT[v][:, h * 256 : (h + 1) * 256, :].rearrange("p n j -> p (n j)").bitcast(F32)
+            i = xt[v, h][:].rearrange("p t u r -> p t r u")
+            o = o.rearrange("p (t r u) -> p t r u", t=2, u=2)
+            if eng == "s":
+                nc.scalar.copy(o, i)
+            else:
+                nc.vector.tensor_copy(out=o, in_=i)
+
+        def QS(v):
+            s_codes[v] = sbuf(work, [P, N], U32, "s_codes", 3)
+            s_scales[v] = sbuf(work, [P, N], U8, "s_scales", 3)
+            nc.vector.quantize_mx(out=s_codes[v][:].bitcast(FP8X4), scales=s_scales[v][:],
+                                  in_=sT[v][:].rearrange("p n j -> p (n j)"))
+
+        t3 = [None] * J
+
+        def T3(v, first, last):
+            for tj in range(J):
+                if first:
+                    t3[tj] = bank([P, J, P], "t3")
+                nc.tensor.matmul(t3[tj][:], lhsT=ident_bf[:], rhs=p_sb[v][:, :, tj::J], start=first, stop=last)
+
+        tot = sbuf(keep, [P, J, P, J], F32, "tot", 1)
+
+        def pv(v):
+            return p_sb[v][:].rearrange("p k (m t) -> p t m k", t=J)
+
+        def TOT(tj):
+            nc.vector.tensor_tensor(out=tot[:, tj], in0=t3[tj][:].rearrange("p k m -> p m k"), in1=pv(0)[:, tj], op=ADD)
+
+        m_bf, m_codes, m_scales, x = {}, {}, {}, {}
+
+        def m_tile(v):
+            if v not in m_bf:
+                m_bf[v] = sbuf(work, [P, J, P, J], BF16, "m_bf", 2)
+            return m_bf[v]
+
+        def M0(tj, eng):
+            o, i = m_tile(0)[:, tj], t3[tj][:].rearrange("p k m -> p m k")
+            if eng == "s":
+                nc.scalar.activation(out=o, in_=i, func=COPY, scale=THIRD)
+            else:
+                nc.vector.tensor_scalar(out=o, in0=i, scalar1=THIRD, scalar2=None, op0=MULT)
+
+        def X(v, tj):
+            if tj == 0:
+                x[v] = sbuf(work, [P, J, P, J], F32, "x", 2)
+            nc.vector.tensor_tensor(out=x[v][:, tj], in0=tot[:, tj], in1=pv(v)[:, tj], op=SUB)
+
+        def XS(v, h):
+            c = slice(2 * h, 2 * h + 2)
+            o, i = m_tile(v)[:, c].rearrange("p t m k -> p (t m k)"), x[v][:, c].rearrange("p t m k -> p (t m k)")
+            if X_ENGINE == "v":
+                nc.vector.tensor_scalar(out=o, in0=i, scalar1=THIRD, scalar2=None, op0=MULT)
+            elif X_ENGINE == "g":
+                nc.gpsimd.tensor_scalar(out=o, in0=i, scalar1=THIRD, scalar2=0.0, op0=MULT, op1=ADD)
+            else:
+                nc.scalar.activation(out=o, in_=i, func=COPY, scale=THIRD)
+
+        def QM(v):
+            m_codes[v] = sbuf(work, [P, N], U32, "m_codes", 2)
+            m_scales[v] = sbuf(work, [P, N], U8, "m_scales", 2)
+            nc.vector.quantize_mx(out=m_codes[v][:].bitcast(FP8X4), scales=m_scales[v][:],
+                                  in_=m_bf[v][:].rearrange("p t m k -> p (t m k)"))
+
+        tb, tT, t_codes, t_scales = {}, {}, {}, {}
+
+        def ST1(v, ib):
+            b = bank([P, J, P], "tb")
+            for tj in range(J):
+                a, c = slice(tj * P, (tj + 1) * P), slice(ib * P, (ib + 1) * P)
+                nc.tensor.matmul_mx(out=b[:, tj, :], lhsT=m_codes[v][:, a].bitcast(FP8X4), lhsT_scale=m_scales[v][:, a],
+                                    rhs=s_codes[v][:, c].bitcast(FP8X4), rhs_scale=s_scales[v][:, c], start=True, stop=True)
+            tb[v, ib] = b
+
+        def TC(v, ib, eng):
+            if ib == 0:
+                tT[v] = sbuf(work, [P, N, J], BF16, "tT", 2)
+            o, i = tT[v][:, ib * P : (ib + 1) * P, :], tb[v, ib][:].rearrange("p t n -> p n t")
+            if eng == "s":
+                nc.scalar.copy(o, i)
+            else:
+                nc.vector.tensor_copy(out=o, in_=i)
+
+        def QT(v, h):
+            if h == 0:
+                t_codes[v] = sbuf(work, [P, N], U32, "t_codes", 2)
+                t_scales[v] = sbuf(work, [P, N], U8, "t_scales", 2)
+            c = slice(h * 256, (h + 1) * 256)
+            nc.vector.quantize_mx(out=t_codes[v][:, c].bitcast(FP8X4), scales=t_scales[v][:, c],
+                                  in_=tT[v][:, c, :].rearrange("p n j -> p (n j)"))
+
+        q = {}
+
+        def ST2(v, t):
+            b = bank([P, N], "q")
+            a = slice(t * P, (t + 1) * P)
+            nc.tensor.matmul_mx(out=b[:], lhsT=t_codes[v][:, a].bitcast(FP8X4), lhsT_scale=t_scales[v][:, a],
+                                rhs=s_codes[v][:].bitcast(FP8X4), rhs_scale=s_scales[v][:], start=True, stop=True)
+            q[v, t] = b
+
+        dsum, g, r = {}, {}, {}
+
+        def A(v, t):
+            if t == 0:
+                dsum[v] = sbuf(work, [P, J], F32, "dsum", 2)
+            junk = sbuf(work, [P, N], F32, "junk", 2)
+            nc.scalar.activation(out=junk[:], in_=q[v, t][:], func=ABS, scale=2.0 / N, accum_out=dsum[v][:, t : t + 1])
+
+        ee = {}
+
+        def GE(v):
+            ee[v] = sbuf(work, [P, J], F32, "ee", 2)
+            nc.vector.tensor_scalar(out=ee[v][:], in0=dsum[v][:], scalar1=2e-6, scalar2=None, op0=ADD)
+
+        def GR(v):
+            g[v] = sbuf(work, [P, J], F32, "g", 2)
+            nc.vector.reciprocal(out=g[v][:], in_=ee[v][:])
+
+        def B(v, t, eng):
+            if t == 0:
+                r[v] = sbuf(work, [P, J, N], F32, "r", 2)
+            gc = g[v][:, t : t + 1]
+            if eng == "s":
+                nc.scalar.activation(out=r[v][:, t, :], in_=q[v, t][:], func=COPY, scale=gc)
+            else:
+                nc.vector.tensor_scalar(out=r[v][:, t, :], in0=q[v, t][:], scalar1=gc, scalar2=None, op0=MULT)
+
+        rt = {}
+
+        def RT(v, t):
+            b = bank([P, J, P], "rt")
+            for t2 in range(J):
+                nc.tensor.transpose(b[:, t2, :], r[v][:, t2, t * P : (t + 1) * P], ident[:])
+            rt[v, t] = b
+
+        o_sb, pb, p_codes, p_scales = {}, {}, {}, {}
+
+        def C(v, t, h, nh):
+            if v not in o_sb:
+                o_sb[v] = sbuf(work, [P, J, N], F32, "o_sb", 3)
+            w = P // nh
+            c = slice(h * w, (h + 1) * w)
+            nc.vector.tensor_tensor(out=o_sb[v][:, t, h * w * J : (h + 1) * w * J].rearrange("p (q t) -> p q t", t=J),
+                                    in0=rt[v, t][:, :, c].rearrange("p t q -> p q t"),
+                                    in1=r[v][:, t, :].rearrange("p (t q) -> p q t", t=J)[:, c, :], op=ADD)
+
+        def SO(v, t):
+            nc.sync.dma_start(out=out_0[v].rearrange("(p t) l -> p t l", t=J)[:, t, :], in_=o_sb[v][:, t, :])
+
+        def D(v, h, nh, eng):
+            if v not in pb:
+                pb[v] = sbuf(work, [P, N, J], BF16, "pb", 2)
+            w = N // nh
+            c = slice(h * w, (h + 1) * w)
+            o, i = pb[v][:, c, :], o_sb[v][:, :, c].rearrange("p t l -> p l t")
+            if eng == "s":
+                nc.scalar.copy(o, i)
+            elif eng == "v":
+                nc.vector.tensor_copy(out=o, in_=i)
+            else:
+                nc.gpsimd.tensor_scalar(out=o, in0=i, scalar1=1.0, scalar2=0.0, op0=MULT, op1=ADD)
+
+        def QP(v, h, nh):
+            if v not in p_codes:
+                p_codes[v] = sbuf(work, [P, N], U32, "p_codes", 2)
+                p_scales[v] = sbuf(work, [P, N], U8, "p_scales", 2)
+            w = N // nh
+            c = slice(h * w, (h + 1) * w)
+            nc.vector.quantize_mx(out=p_codes[v][:, c].bitcast(FP8X4), scales=p_scales[v][:, c],
+                                  in_=pb[v][:, c, :].rearrange("p n j -> p (n j)"))
+
+        def SP(v, h, nh):
+            w = N // nh
+            c = slice(h * w, (h + 1) * w)
+            nc.sync.dma_start(out=words[:, v * N + h * w : v * N + (h + 1) * w], in_=p_codes[v][:, c].bitcast(I32))
+            for Q in range(4):
+                nc.sync.dma_start(out=scale_rows[4 * Q : 4 * Q + 4, (v * N + h * w) // 4 : (v * N + (h + 1) * w) // 4],
+                                  in_=p_scales[v][32 * Q : 32 * Q + 4, c].bitcast(I32))
+
+        XT(0)
+        XC(0, 0, "s")
+        XC(0, 1, "s")
+        QS(0)
+        T3(1, True, False)
+        T3(2, False, False)
+        T3(3, False, True)
+        M0(0, "s")
+        M0(2, "v")
+        M0(1, "s")
+        M0(3, "v")
+        XT(1)
+        TOT(0)
+        QM(0)
+        for ib in range(J):
+            ST1(0, ib)
+        for tj in range(1, J):
+            TOT(tj)
+        XC(1, 0, "s")
+        XC(1, 1, "s")
+
+        for v in range(V):
+            last = v == V - 1
+            if v > 0:
+                C(v - 1, 0, 0, 1)
+            TC(v, 0, "s")
+            TC(v, 1, "s")
+            QT(v, 0)
+            ST2(v, 0)
+            ST2(v, 1)
+            if v > 0:
+                C(v - 1, 1, 0, 1)
+            TC(v, 2, "s" if not last else "v")
+            TC(v, 3, "s")
+            QT(v, 1)
+            ST2(v, 2)
+            ST2(v, 3)
+            if v > 0:
+                C(v - 1, 2, 0, 1)
+                C(v - 1, 3, 0, 1)
+                for t in range(J):
+                    SO(v - 1, t)
+            if v == 0:
+                QS(1)
+            A(v, 0)
+            A(v, 1)
+            A(v, 2)
+            A(v, 3)
+            if v + 2 < V:
+                XT(v + 2)
+                XC(v + 2, 0, "s")
+                XC(v + 2, 1, "s")
+            if not last:
+                X(v + 1, 0)
+                GE(v)
+                X(v + 1, 1)
+                GR(v)
+                X(v + 1, 2)
+                XS(v + 1, 0)
+                X(v + 1, 3)
+                if v + 2 < V:
+                    QS(v + 2)
+                XS(v + 1, 1)
+                if v > 0:
+                    D(v - 1, 1, 2, "v")
+                QM(v + 1)
+                for t in range(J):
+                    B(v, t, "s")
+                RT(v, 0)
+                RT(v, 1)
+                for ib in range(J):
+                    ST1(v + 1, ib)
+                RT(v, 2)
+                RT(v, 3)
+                if v > 0:
+                    D(v - 1, 0, 2, "s")
+                    QP(v - 1, 0, 1)
+                    SP(v - 1, 0, 1)
+            else:
+                D(v - 1, 0, 2, "v")
+                GE(v)
+                D(v - 1, 1, 2, "v")
+                GR(v)
+                QP(v - 1, 0, 1)
+                SP(v - 1, 0, 1)
+                B(v, 0, "s")
+                B(v, 2, "v")
+                B(v, 1, "s")
+                B(v, 3, "v")
+                for t in range(J):
+                    RT(v, t)
+
+        v = V - 1
+        for h in range(2):
+            for t in range(J):
+                C(v, t, h, 2)
+                if h == 1:
+                    SO(v, t)
+            if h == 0:
+                D(v, 0, 2, "s")
+                continue
+            D(v, 2, 4, "s")
+            D(v, 3, 4, "v")
+            QP(v, 0, 2)
+            SP(v, 0, 2)
+            QP(v, 1, 2)
+            SP(v, 1, 2)

@@ -6,8 +6,9 @@ from concourse.masks import make_identity
 V, N = 4, 512
 P = 128
 J = 4
-FLOPS = 2 * V * 2 * N * N * N
-BYTES = 2 * V * N * N * 2 + V * N * N * 4 + P * V * N * 4 + 16 * V * N
+
+FLOPS = V * 2 * 2 * N * N * N
+BYTES = 2 * V * N * N * 2 + V * N * N * 4 + P * V * N * J + 16 * V * N
 
 F32 = mybir.dt.float32
 BF16 = mybir.dt.bfloat16
@@ -15,359 +16,349 @@ U32 = mybir.dt.uint32
 I32 = mybir.dt.int32
 U8 = mybir.dt.uint8
 FP8X4 = mybir.dt.float8_e4m3fn_x4
-ADD = mybir.AluOpType.add
-SUB = mybir.AluOpType.subtract
-MULT = mybir.AluOpType.mult
-COPY = mybir.ActivationFunctionType.Copy
-ABS = mybir.ActivationFunctionType.Abs
+ADD, SUBTRACT, MULT = mybir.AluOpType.add, mybir.AluOpType.subtract, mybir.AluOpType.mult
+COPY, ABS = mybir.ActivationFunctionType.Copy, mybir.ActivationFunctionType.Abs
 
 THIRD = 1.0 / 3.0
-MANUAL = True
-X_ENGINE = "v"
+EPS = 1e-6
+LAST = V - 1
+
+TENSOR = [
+    ("warm_up", 0, 9), ("sum", 1, 2), ("turn", 0, 2), ("sum", 2, 2), ("sum", 1, 1), ("sum", 3, 1), ("sum", 2, 1),
+    ("sum", 3, 1), ("sum", 1, 1), ("sum", 3, 1), ("sum", 2, 1), ("sum", 3, 1), ("turn", 1, 2), ("mm1", 0, 4),
+    ("mm2", 0, 4), ("turn", 2, 2), ("mm1", 1, 4), ("mm2", 1, 2), ("mm1", 2, 2), ("mm2", 1, 1),
+    ("flip", 0, 1), ("mm2", 1, 1), ("mm1", 2, 2), ("turn", 3, 1), ("flip", 0, 1), ("turn", 3, 1), ("mm2", 2, 3),
+    ("mm1", 3, 1), ("mm2", 2, 1), ("mm1", 3, 3), ("flip", 0, 2), ("flip", 1, 1), ("mm2", 3, 3), ("flip", 1, 1),
+    ("mm2", 3, 1), ("flip", 1, 2), ("flip", 2, 4), ("flip", 3, 4),
+]
+SCALAR = [
+    ("turn_out", 0, 2), ("mean0", 0, 4), ("turn_out", 1, 2), ("t_out", 0, 4), ("magnitude", 0, 4), ("turn_out", 2, 2),
+    ("scale", 0, 4), ("t_out", 1, 4), ("magnitude", 1, 2), ("t_out", 2, 2), ("magnitude", 1, 2), ("t_out", 2, 2), ("scale", 1, 2),
+    ("turn_out", 3, 2), ("magnitude", 2, 4), ("t_out", 3, 2), ("scale", 2, 3), ("magnitude", 3, 4), ("cast", 0, 1),
+    ("scale", 3, 4), ("cast", 1, 1), ("cast", 2, 1), ("cast", 1, 1), ("cast", 3, 1), ("cast", 2, 1),
+]
+VECTOR = [
+    ("quant_s", 0, 1), ("total", 0, 3), ("quant_m", 0, 1), ("others", 2, 1), ("others", 1, 1), ("quant_t", 0, 1),
+    ("total", 0, 1), ("quant_t", 0, 1), ("others", 3, 1), ("others", 1, 1), ("divisor", 0, 1), ("mean", 1, 1),
+    ("gain", 0, 1), ("mean", 1, 1), ("quant_s", 1, 1), ("quant_m", 1, 1), ("others", 2, 1), ("mean", 2, 2),
+    ("quant_t", 1, 1), ("quant_m", 2, 1), ("quant_s", 2, 1), ("quant_t", 1, 1), ("others", 3, 1), ("join", 0, 1),
+    ("mean", 3, 1), ("divisor", 1, 1), ("quant_t", 2, 1), ("gain", 1, 1), ("mean", 3, 1), ("scale", 1, 2),
+    ("quant_t", 2, 1), ("quant_m", 3, 1), ("quant_s", 3, 1), ("join", 0, 1), ("t_out", 3, 2), ("divisor", 2, 1),
+    ("gain", 2, 1), ("quant_t", 3, 1), ("scale", 2, 1), ("quant_t", 3, 1), ("join", 0, 2), ("join", 1, 1),
+    ("cast", 0, 1), ("join", 1, 1), ("divisor", 3, 1), ("join", 1, 1), ("gain", 3, 1), ("join", 1, 1), ("join", 2, 4),
+    ("quant_out", 0, 2), ("join", 3, 1), ("quant_out", 1, 1), ("join", 3, 2), ("quant_out", 2, 1), ("join", 3, 5),
+    ("quant_out", 1, 1), ("cast", 3, 1, 1), ("quant_out", 3, 2), ("quant_out", 2, 1),
+]
+
+
+def expand(runs, counts):
+    steps = []
+    for stage, v, length, *first in runs:
+        if not first:
+            first = [counts.get((stage, v), 0)]
+            counts[stage, v] = first[0] + length
+        steps.extend((stage, v, first[0] + k) for k in range(length))
+    return steps
+
+
+def reads(stage, v, i):
+    halves, quarters = range(2), range(J)
+    two = (2 * i, 2 * i + 1)
+    if stage == "turn_out":
+        return [("turn", v, i)]
+    if stage == "quant_s":
+        return [("turn_out", v, k) for k in halves]
+    if stage == "sum" and v > 1:
+        return [("sum", v - 1, i)]
+    if stage == "mean0" or stage == "total":
+        return [("sum", LAST, i)]
+    if stage == "others":
+        return [("total", 0, k) for k in two]
+    if stage == "mean":
+        return [("others", v, i)]
+    if stage == "quant_m":
+        return [("mean0", 0, k) for k in quarters] if v == 0 else [("mean", v, k) for k in halves]
+    if stage == "mm1":
+        return [("quant_m", v, 0), ("quant_s", v, 0)]
+    if stage == "t_out":
+        return [("mm1", v, i)]
+    if stage == "quant_t":
+        return [("t_out", v, k) for k in two]
+    if stage == "mm2":
+        return [("quant_t", v, i // 2)]
+    if stage == "magnitude":
+        return [("mm2", v, i)]
+    if stage == "divisor":
+        return [("magnitude", v, k) for k in quarters]
+    if stage == "gain":
+        return [("divisor", v, 0)]
+    if stage == "scale":
+        return [("gain", v, 0)]
+    if stage == "flip":
+        return [("scale", v, k) for k in quarters]
+    if stage == "join":
+        return [("flip", v, i % J)]
+    if stage == "cast":
+        return [("join", v, k + (J * i if v == LAST else 0)) for k in quarters]
+    if stage == "quant_out":
+        return [("cast", v, i)]
+    return []
 
 
 def tile_signedsimilaritynetworkcrossdiffusion_x1_kernel(tc, s, p, out_0, out_1, out_2):
     nc = tc.nc
-    words = out_1[0].rearrange("p m t -> p (m t)").bitcast(I32)
-    scale_rows = out_2[0].bitcast(I32)
+    out_words = out_1[0].rearrange("b m n -> b (m n)").bitcast(I32)
+    out_scales = out_2[0].bitcast(I32)
 
     with ExitStack() as ctx:
-        keep = ctx.enter_context(tc.tile_pool(name="keep", bufs=1))
-        work = ctx.enter_context(tc.tile_pool(name="work", bufs=2))
-        psum = ctx.enter_context(tc.psum_pool(name="psum", bufs=8))
-        if MANUAL:
-            ctx.enter_context(tc.manual_schedule())
+        pool = ctx.enter_context(tc.tile_pool(name="pool", bufs=1))
+        psum = ctx.enter_context(tc.psum_pool(name="psum", bufs=4))
+        ctx.enter_context(tc.manual_schedule())
+        made = {}
 
-        def bank(shape, name):
-            return psum.tile(shape, F32, name=name, tag="bank")
+        def sbuf(name, v, shape, dt, bufs):
+            if (name, v) not in made:
+                made[name, v] = pool.tile(shape, dt, name=name, tag=name, bufs=bufs, align_bytes=64)
+            return made[name, v]
 
-        def sbuf(pool, shape, dt, name, bufs):
-            return pool.tile(shape, dt, name=name, tag=name, bufs=bufs, align_bytes=64)
+        def bank(name, v, i, *shape):
+            if (name, v, i) not in made:
+                tag = "read_again" if name in ("sum", "q") else "read_once"
+                made[name, v, i] = psum.tile([P] + list(shape), F32, name=name, tag=tag, bufs=4)
+            return made[name, v, i]
 
-        s_sb, p_sb = [None] * V, [None] * V
+        def s_rows(v):
+            return sbuf("s_rows" + str(v), v, [P, J, N], BF16, 1)
 
-        def load_s(v, pieces):
-            s_sb[v] = sbuf(keep, [P, J, N], BF16, "s_sb" + str(v), 1)
-            src = s[v].rearrange("(p t) k -> p t k", t=J)
-            step = J // pieces
-            for t in range(0, J, step):
-                nc.sync.dma_start(out=s_sb[v][:, t : t + step, :], in_=src[:, t : t + step, :])
+        def p_rows(v):
+            return sbuf("p_rows" + str(v), v, [P, J, N], BF16, 1)
 
-        def load_p(v):
-            p_sb[v] = sbuf(keep, [P, J, N], BF16, "p_sb" + str(v), 1)
-            nc.sync.dma_start(out=p_sb[v][:], in_=p[v].rearrange("(p t) j -> p t j", t=J))
+        def quantised(name, v):
+            return sbuf(name + "_codes", v, [P, N], U32, 4), sbuf(name + "_scales", v, [P, N], U8, 4)
 
-        load_s(0, 2)
-        for v in (1, 2, 3, 0):
-            load_p(v)
+        def s_turned(v):
+            return sbuf("s_turned", v, [P, N, J], BF16, 3)
+
+        def total():
+            return sbuf("total", 0, [P, J, P, J], F32, 1)
+
+        def others(v):
+            return sbuf("others", v, [P, J, P, J], F32, 3)
+
+        def mean(v):
+            return sbuf("mean", v, [P, J, P, J], BF16, 3)
+
+        def t_turned(v):
+            return sbuf("t_turned", v, [P, N, J], BF16, 3)
+
+        def column(name, v):
+            return sbuf(name, v, [P, J], F32, 4)
+
+        def scaled(v):
+            return sbuf("scaled", v, [P, J, N], F32, 3)
+
+        def result(v):
+            return sbuf("result", v, [P, J, N], F32, 4)
+
+        def rounded(v):
+            return sbuf("rounded", v, [P, N, J], BF16, 3)
+
+        def result_codes(v):
+            return sbuf("result_codes", v, [P, N], U32, 4)
+
+        def result_scales():
+            return sbuf("result_scales", 0, [P, V * N], U8, 1)
+
+        def chunk(i, width=P):
+            return slice(i * width, (i + 1) * width)
+
+        def copy(engine, out, in_):
+            if engine == "scalar":
+                nc.scalar.copy(out, in_)
+            else:
+                nc.vector.tensor_copy(out=out, in_=in_)
+
+        def times(engine, out, in_, factor):
+            if engine == "scalar":
+                nc.scalar.activation(out=out, in_=in_, func=COPY, scale=factor)
+            else:
+                nc.vector.tensor_scalar(out=out, in0=in_, scalar1=factor, scalar2=None, op0=MULT)
+
+        def quantize(code_words, scale_bytes, values):
+            nc.vector.quantize_mx(out=code_words.bitcast(FP8X4), scales=scale_bytes, in_=values)
+
+        def product(out, left, left_columns, right, right_columns):
+            nc.tensor.matmul_mx(
+                out=out,
+                lhsT=left[0][:, left_columns].bitcast(FP8X4),
+                lhsT_scale=left[1][:, left_columns],
+                rhs=right[0][:, right_columns].bitcast(FP8X4),
+                rhs_scale=right[1][:, right_columns],
+                start=True,
+                stop=True,
+            )
+
+
+        def warm_up(v, i, engine):
+            flat = bank("sum", 0, 0, J, P)[:].rearrange("b k a -> b (k a)")
+            product(flat[:, chunk(0, 2 * P)], zeros, chunk(0), zeros, chunk(0, 2 * P))
+
+        def turn(v, i, engine):
+            words = s_rows(v)[:].bitcast(F32)
+            for n in range(2):
+                for w in range(2):
+                    nc.tensor.transpose(bank("s", v, i, 2, 2, P)[:, n, w, :], words[:, 2 * i + n, w::2], identity[:])
+
+        def turn_out(v, i, engine):
+            out = s_turned(v)[:, chunk(i, 2 * P), :].rearrange("b c k -> b (c k)").bitcast(F32)
+            copy(engine, out.rearrange("b (n a w) -> b n a w", n=2, w=2), bank("s", v, i)[:].rearrange("b n w a -> b n a w"))
+
+        def quant_s(v, i, engine):
+            codes, scales = quantised("s", v)
+            quantize(codes[:], scales[:], s_turned(v)[:].rearrange("b c k -> b (c k)"))
+
+        def sum_p(v, i, engine):
+            columns = p_rows(v)[:, :, i::J]
+            nc.tensor.matmul(bank("sum", 0, i, J, P)[:], lhsT=identity_bf[:], rhs=columns, start=(v == 1), stop=(v == LAST))
+
+        def mean_0(v, i, engine):
+            times(engine, mean(0)[:, i], bank("sum", 0, i)[:].rearrange("b k a -> b a k"), THIRD)
+
+        def add_p0(v, i, engine):
+            nc.vector.tensor_tensor(
+                out=total()[:, i],
+                in0=bank("sum", 0, i)[:].rearrange("b k a -> b a k"),
+                in1=p_rows(0)[:, :, i::J].rearrange("b k a -> b a k"),
+                op=ADD,
+            )
+
+        def subtract_own(v, i, engine):
+            own = p_rows(v)[:].rearrange("b k (a n) -> b n a k", n=J)
+            two = chunk(i, 2)
+            nc.vector.tensor_tensor(out=others(v)[:, two], in0=total()[:, two], in1=own[:, two], op=SUBTRACT)
+
+        def take_third(v, i, engine):
+            flat, two = "b n a k -> b (n a k)", chunk(i, 2)
+            times(engine, mean(v)[:, two].rearrange(flat), others(v)[:, two].rearrange(flat), THIRD)
+
+        def quant_m(v, i, engine):
+            codes, scales = quantised("m", v)
+            quantize(codes[:], scales[:], mean(v)[:].rearrange("b n a k -> b (n a k)"))
+
+        def mm1(v, i, engine):
+            for n in range(J):
+                product(bank("t", v, i, J, P)[:, n, :], quantised("m", v), chunk(n), quantised("s", v), chunk(i))
+
+        def t_out(v, i, engine):
+            copy(engine, t_turned(v)[:, chunk(i), :], bank("t", v, i)[:].rearrange("b n a -> b a n"))
+
+        def quant_t(v, i, engine):
+            (codes, scales), half = quantised("t", v), chunk(i, 2 * P)
+            quantize(codes[:, half], scales[:, half], t_turned(v)[:, half, :].rearrange("b c k -> b (c k)"))
+
+        def mm2(v, i, engine):
+            product(bank("q", v, i, N)[:], quantised("t", v), chunk(i), quantised("s", v), chunk(0, N))
+
+        def magnitude(v, i, engine):
+            written = sbuf("magnitudes", (v, i), [P, N], F32, 2)
+            sums = column("two_d", v)[:, i : i + 1]
+            nc.scalar.activation(out=written[:], in_=bank("q", v, i)[:], func=ABS, scale=2.0 / N, accum_out=sums)
+
+        def divisor(v, i, engine):
+            out = column("divisor", v)
+            nc.vector.tensor_scalar(out=out[:], in0=column("two_d", v)[:], scalar1=2 * EPS, scalar2=None, op0=ADD)
+
+        def gain(v, i, engine):
+            nc.vector.reciprocal(out=column("gain", v)[:], in_=column("divisor", v)[:])
+
+        def scale(v, i, engine):
+            times(engine, scaled(v)[:, i, :], bank("q", v, i)[:], column("gain", v)[:, i : i + 1])
+
+        def flip(v, i, engine):
+            for n in range(J):
+                nc.tensor.transpose(bank("flip", v, i, J, P)[:, n, :], scaled(v)[:, n, chunk(i)], identity[:])
+
+        def join(v, i, engine):
+            parts = 2 if v == LAST else 1
+            n, part = i % J, i // J
+            a, columns = chunk(part, P // parts), chunk(part, N // parts)
+            nc.vector.tensor_tensor(
+                out=result(v)[:, n, columns].rearrange("b (a k) -> b a k", k=J),
+                in0=bank("flip", v, n)[:, :, a].rearrange("b k a -> b a k"),
+                in1=scaled(v)[:, n, :].rearrange("b (k a) -> b a k", k=J)[:, a, :],
+                op=ADD,
+            )
+            if n == J - 1:
+                rows = out_0[v].rearrange("(b n) l -> b n l", n=J)
+                nc.sync.dma_start(out=rows[:, :, columns], in_=result(v)[:, :, columns])
+
+        def cast(v, i, engine):
+            half = chunk(i, N // 2)
+            copy(engine, rounded(v)[:, half, :], result(v)[:, :, half].rearrange("b n l -> b l n"))
+
+        def quant_out(v, i, engine):
+            half, place = chunk(i, N // 2), chunk(2 * v + i, N // 2)
+            quantize(result_codes(v)[:, half], result_scales()[:, place], rounded(v)[:, half, :].rearrange("b l n -> b (l n)"))
+            nc.sync.dma_start(out=out_words[:, place], in_=result_codes(v)[:, half].bitcast(I32))
+
+        do = {
+            "warm_up": warm_up,
+            "turn": turn,
+            "turn_out": turn_out,
+            "quant_s": quant_s,
+            "sum": sum_p,
+            "mean0": mean_0,
+            "total": add_p0,
+            "others": subtract_own,
+            "mean": take_third,
+            "quant_m": quant_m,
+            "mm1": mm1,
+            "t_out": t_out,
+            "quant_t": quant_t,
+            "mm2": mm2,
+            "magnitude": magnitude,
+            "divisor": divisor,
+            "gain": gain,
+            "scale": scale,
+            "flip": flip,
+            "join": join,
+            "cast": cast,
+            "quant_out": quant_out,
+        }
+
+        def load(tile, source, first, count):
+            neighbours = slice(first, first + count)
+            nc.sync.dma_start(out=tile[:, neighbours, :], in_=source.rearrange("(b n) k -> b n k", n=J)[:, neighbours, :])
+
+        load(p_rows(1), p[1], 0, J)
+        for first in (0, 2):
+            load(s_rows(0), s[0], first, 2)
+        for v in (2, 3, 0):
+            load(p_rows(v), p[v], 0, J)
         for v in range(1, V):
-            load_s(v, 1)
+            load(s_rows(v), s[v], 0, J)
 
-        ident = sbuf(keep, [P, P], F32, "ident", 1)
-        make_identity(nc, ident[:])
-        ident_bf = sbuf(keep, [P, P], BF16, "ident_bf", 1)
-        make_identity(nc, ident_bf[:])
+        identity = sbuf("identity", 0, [P, P], F32, 1)
+        identity_bf = sbuf("identity_bf", 0, [P, P], BF16, 1)
+        make_identity(nc, identity_bf[:])
+        make_identity(nc, identity[:])
 
-        xt = {}
-        s_codes, s_scales = {}, {}
-        sT = {}
+        zero_rows = sbuf("zero_rows", 0, [P, 2 * P * J], BF16, 1)
+        zeros = sbuf("zero_codes", 0, [P, 2 * P], U32, 1), sbuf("zero_scales", 0, [P, 2 * P], U8, 1)
+        nc.vector.memset(zero_rows[:], 0.0)
+        quantize(zeros[0][:], zeros[1][:], zero_rows[:])
 
-        def XT(v):
-            w = s_sb[v][:].bitcast(F32)
-            for h in range(2):
-                b = bank([P, 2, 2, P], "xt")
-                for tt in range(2):
-                    for u in range(2):
-                        nc.tensor.transpose(b[:, tt, u, :], w[:, 2 * h + tt, u::2], ident[:])
-                xt[v, h] = b
+        counts = {}
+        queues = [("vector", expand(VECTOR, counts)), ("scalar", expand(SCALAR, counts)), ("tensor", expand(TENSOR, counts))]
+        written = set()
+        while any(steps for engine, steps in queues):
+            for engine, steps in queues:
+                while steps and all(step in written for step in reads(*steps[0])):
+                    stage, v, i = steps[0]
+                    do[stage](v, i, engine)
+                    written.add(steps[0])
+                    steps.remove(steps[0])
 
-        def XC(v, h, eng):
-            if h == 0:
-                sT[v] = sbuf(work, [P, N, J], BF16, "sT", 2)
-            o = sT[v][:, h * 256 : (h + 1) * 256, :].rearrange("p n j -> p (n j)").bitcast(F32)
-            i = xt[v, h][:].rearrange("p t u r -> p t r u")
-            o = o.rearrange("p (t r u) -> p t r u", t=2, u=2)
-            if eng == "s":
-                nc.scalar.copy(o, i)
-            else:
-                nc.vector.tensor_copy(out=o, in_=i)
-
-        def QS(v):
-            s_codes[v] = sbuf(work, [P, N], U32, "s_codes", 3)
-            s_scales[v] = sbuf(work, [P, N], U8, "s_scales", 3)
-            nc.vector.quantize_mx(out=s_codes[v][:].bitcast(FP8X4), scales=s_scales[v][:],
-                                  in_=sT[v][:].rearrange("p n j -> p (n j)"))
-
-        t3 = [None] * J
-
-        def T3(v, first, last):
-            for tj in range(J):
-                if first:
-                    t3[tj] = bank([P, J, P], "t3")
-                nc.tensor.matmul(t3[tj][:], lhsT=ident_bf[:], rhs=p_sb[v][:, :, tj::J], start=first, stop=last)
-
-        tot = sbuf(keep, [P, J, P, J], F32, "tot", 1)
-
-        def pv(v):
-            return p_sb[v][:].rearrange("p k (m t) -> p t m k", t=J)
-
-        def TOT(tj):
-            nc.vector.tensor_tensor(out=tot[:, tj], in0=t3[tj][:].rearrange("p k m -> p m k"), in1=pv(0)[:, tj], op=ADD)
-
-        m_bf, m_codes, m_scales, x = {}, {}, {}, {}
-
-        def m_tile(v):
-            if v not in m_bf:
-                m_bf[v] = sbuf(work, [P, J, P, J], BF16, "m_bf", 2)
-            return m_bf[v]
-
-        def M0(tj, eng):
-            o, i = m_tile(0)[:, tj], t3[tj][:].rearrange("p k m -> p m k")
-            if eng == "s":
-                nc.scalar.activation(out=o, in_=i, func=COPY, scale=THIRD)
-            else:
-                nc.vector.tensor_scalar(out=o, in0=i, scalar1=THIRD, scalar2=None, op0=MULT)
-
-        def X(v, tj):
-            if tj == 0:
-                x[v] = sbuf(work, [P, J, P, J], F32, "x", 2)
-            nc.vector.tensor_tensor(out=x[v][:, tj], in0=tot[:, tj], in1=pv(v)[:, tj], op=SUB)
-
-        def XS(v, h):
-            c = slice(2 * h, 2 * h + 2)
-            o, i = m_tile(v)[:, c].rearrange("p t m k -> p (t m k)"), x[v][:, c].rearrange("p t m k -> p (t m k)")
-            if X_ENGINE == "v":
-                nc.vector.tensor_scalar(out=o, in0=i, scalar1=THIRD, scalar2=None, op0=MULT)
-            elif X_ENGINE == "g":
-                nc.gpsimd.tensor_scalar(out=o, in0=i, scalar1=THIRD, scalar2=0.0, op0=MULT, op1=ADD)
-            else:
-                nc.scalar.activation(out=o, in_=i, func=COPY, scale=THIRD)
-
-        def QM(v):
-            m_codes[v] = sbuf(work, [P, N], U32, "m_codes", 2)
-            m_scales[v] = sbuf(work, [P, N], U8, "m_scales", 2)
-            nc.vector.quantize_mx(out=m_codes[v][:].bitcast(FP8X4), scales=m_scales[v][:],
-                                  in_=m_bf[v][:].rearrange("p t m k -> p (t m k)"))
-
-        tb, tT, t_codes, t_scales = {}, {}, {}, {}
-
-        def ST1(v, ib):
-            b = bank([P, J, P], "tb")
-            for tj in range(J):
-                a, c = slice(tj * P, (tj + 1) * P), slice(ib * P, (ib + 1) * P)
-                nc.tensor.matmul_mx(out=b[:, tj, :], lhsT=m_codes[v][:, a].bitcast(FP8X4), lhsT_scale=m_scales[v][:, a],
-                                    rhs=s_codes[v][:, c].bitcast(FP8X4), rhs_scale=s_scales[v][:, c], start=True, stop=True)
-            tb[v, ib] = b
-
-        def TC(v, ib, eng):
-            if ib == 0:
-                tT[v] = sbuf(work, [P, N, J], BF16, "tT", 2)
-            o, i = tT[v][:, ib * P : (ib + 1) * P, :], tb[v, ib][:].rearrange("p t n -> p n t")
-            if eng == "s":
-                nc.scalar.copy(o, i)
-            else:
-                nc.vector.tensor_copy(out=o, in_=i)
-
-        def QT(v, h):
-            if h == 0:
-                t_codes[v] = sbuf(work, [P, N], U32, "t_codes", 2)
-                t_scales[v] = sbuf(work, [P, N], U8, "t_scales", 2)
-            c = slice(h * 256, (h + 1) * 256)
-            nc.vector.quantize_mx(out=t_codes[v][:, c].bitcast(FP8X4), scales=t_scales[v][:, c],
-                                  in_=tT[v][:, c, :].rearrange("p n j -> p (n j)"))
-
-        q = {}
-
-        def ST2(v, t):
-            b = bank([P, N], "q")
-            a = slice(t * P, (t + 1) * P)
-            nc.tensor.matmul_mx(out=b[:], lhsT=t_codes[v][:, a].bitcast(FP8X4), lhsT_scale=t_scales[v][:, a],
-                                rhs=s_codes[v][:].bitcast(FP8X4), rhs_scale=s_scales[v][:], start=True, stop=True)
-            q[v, t] = b
-
-        dsum, g, r = {}, {}, {}
-
-        def A(v, t):
-            if t == 0:
-                dsum[v] = sbuf(work, [P, J], F32, "dsum", 2)
-            junk = sbuf(work, [P, N], F32, "junk", 2)
-            nc.scalar.activation(out=junk[:], in_=q[v, t][:], func=ABS, scale=2.0 / N, accum_out=dsum[v][:, t : t + 1])
-
-        ee = {}
-
-        def GE(v):
-            ee[v] = sbuf(work, [P, J], F32, "ee", 2)
-            nc.vector.tensor_scalar(out=ee[v][:], in0=dsum[v][:], scalar1=2e-6, scalar2=None, op0=ADD)
-
-        def GR(v):
-            g[v] = sbuf(work, [P, J], F32, "g", 2)
-            nc.vector.reciprocal(out=g[v][:], in_=ee[v][:])
-
-        def B(v, t, eng):
-            if t == 0:
-                r[v] = sbuf(work, [P, J, N], F32, "r", 2)
-            gc = g[v][:, t : t + 1]
-            if eng == "s":
-                nc.scalar.activation(out=r[v][:, t, :], in_=q[v, t][:], func=COPY, scale=gc)
-            else:
-                nc.vector.tensor_scalar(out=r[v][:, t, :], in0=q[v, t][:], scalar1=gc, scalar2=None, op0=MULT)
-
-        rt = {}
-
-        def RT(v, t):
-            b = bank([P, J, P], "rt")
-            for t2 in range(J):
-                nc.tensor.transpose(b[:, t2, :], r[v][:, t2, t * P : (t + 1) * P], ident[:])
-            rt[v, t] = b
-
-        o_sb, pb, p_codes, p_scales = {}, {}, {}, {}
-
-        def C(v, t, h, nh):
-            if v not in o_sb:
-                o_sb[v] = sbuf(work, [P, J, N], F32, "o_sb", 3)
-            w = P // nh
-            c = slice(h * w, (h + 1) * w)
-            nc.vector.tensor_tensor(out=o_sb[v][:, t, h * w * J : (h + 1) * w * J].rearrange("p (q t) -> p q t", t=J),
-                                    in0=rt[v, t][:, :, c].rearrange("p t q -> p q t"),
-                                    in1=r[v][:, t, :].rearrange("p (t q) -> p q t", t=J)[:, c, :], op=ADD)
-
-        def SO(v, t):
-            nc.sync.dma_start(out=out_0[v].rearrange("(p t) l -> p t l", t=J)[:, t, :], in_=o_sb[v][:, t, :])
-
-        def D(v, h, nh, eng):
-            if v not in pb:
-                pb[v] = sbuf(work, [P, N, J], BF16, "pb", 2)
-            w = N // nh
-            c = slice(h * w, (h + 1) * w)
-            o, i = pb[v][:, c, :], o_sb[v][:, :, c].rearrange("p t l -> p l t")
-            if eng == "s":
-                nc.scalar.copy(o, i)
-            elif eng == "v":
-                nc.vector.tensor_copy(out=o, in_=i)
-            else:
-                nc.gpsimd.tensor_scalar(out=o, in0=i, scalar1=1.0, scalar2=0.0, op0=MULT, op1=ADD)
-
-        def QP(v, h, nh):
-            if v not in p_codes:
-                p_codes[v] = sbuf(work, [P, N], U32, "p_codes", 2)
-                p_scales[v] = sbuf(work, [P, N], U8, "p_scales", 2)
-            w = N // nh
-            c = slice(h * w, (h + 1) * w)
-            nc.vector.quantize_mx(out=p_codes[v][:, c].bitcast(FP8X4), scales=p_scales[v][:, c],
-                                  in_=pb[v][:, c, :].rearrange("p n j -> p (n j)"))
-
-        def SP(v, h, nh):
-            w = N // nh
-            c = slice(h * w, (h + 1) * w)
-            nc.sync.dma_start(out=words[:, v * N + h * w : v * N + (h + 1) * w], in_=p_codes[v][:, c].bitcast(I32))
-            for Q in range(4):
-                nc.sync.dma_start(out=scale_rows[4 * Q : 4 * Q + 4, (v * N + h * w) // 4 : (v * N + (h + 1) * w) // 4],
-                                  in_=p_scales[v][32 * Q : 32 * Q + 4, c].bitcast(I32))
-
-        XT(0)
-        XC(0, 0, "s")
-        XC(0, 1, "s")
-        QS(0)
-        T3(1, True, False)
-        T3(2, False, False)
-        T3(3, False, True)
-        M0(0, "s")
-        M0(2, "v")
-        M0(1, "s")
-        M0(3, "v")
-        XT(1)
-        TOT(0)
-        QM(0)
-        for ib in range(J):
-            ST1(0, ib)
-        for tj in range(1, J):
-            TOT(tj)
-        XC(1, 0, "s")
-        XC(1, 1, "s")
-
-        for v in range(V):
-            last = v == V - 1
-            if v > 0:
-                C(v - 1, 0, 0, 1)
-            TC(v, 0, "s")
-            TC(v, 1, "s")
-            QT(v, 0)
-            ST2(v, 0)
-            ST2(v, 1)
-            if v > 0:
-                C(v - 1, 1, 0, 1)
-            TC(v, 2, "s" if not last else "v")
-            TC(v, 3, "s")
-            QT(v, 1)
-            ST2(v, 2)
-            ST2(v, 3)
-            if v > 0:
-                C(v - 1, 2, 0, 1)
-                C(v - 1, 3, 0, 1)
-                for t in range(J):
-                    SO(v - 1, t)
-            if v == 0:
-                QS(1)
-            A(v, 0)
-            A(v, 1)
-            A(v, 2)
-            A(v, 3)
-            if v + 2 < V:
-                XT(v + 2)
-                XC(v + 2, 0, "s")
-                XC(v + 2, 1, "s")
-            if not last:
-                X(v + 1, 0)
-                GE(v)
-                X(v + 1, 1)
-                GR(v)
-                X(v + 1, 2)
-                XS(v + 1, 0)
-                X(v + 1, 3)
-                if v + 2 < V:
-                    QS(v + 2)
-                XS(v + 1, 1)
-                if v > 0:
-                    D(v - 1, 1, 2, "v")
-                QM(v + 1)
-                for t in range(J):
-                    B(v, t, "s")
-                RT(v, 0)
-                RT(v, 1)
-                for ib in range(J):
-                    ST1(v + 1, ib)
-                RT(v, 2)
-                RT(v, 3)
-                if v > 0:
-                    D(v - 1, 0, 2, "s")
-                    QP(v - 1, 0, 1)
-                    SP(v - 1, 0, 1)
-            else:
-                D(v - 1, 0, 2, "v")
-                GE(v)
-                D(v - 1, 1, 2, "v")
-                GR(v)
-                QP(v - 1, 0, 1)
-                SP(v - 1, 0, 1)
-                B(v, 0, "s")
-                B(v, 2, "v")
-                B(v, 1, "s")
-                B(v, 3, "v")
-                for t in range(J):
-                    RT(v, t)
-
-        v = V - 1
-        for h in range(2):
-            for t in range(J):
-                C(v, t, h, 2)
-                if h == 1:
-                    SO(v, t)
-            if h == 0:
-                D(v, 0, 2, "s")
-                continue
-            D(v, 2, 4, "s")
-            D(v, 3, 4, "v")
-            QP(v, 0, 2)
-            SP(v, 0, 2)
-            QP(v, 1, 2)
-            SP(v, 1, 2)
+        for Q in range(4):
+            in_ = result_scales()[32 * Q : 32 * Q + 4, :].bitcast(I32)
+            nc.sync.dma_start(out=out_scales[4 * Q : 4 * Q + 4, :], in_=in_)

from contextlib import ExitStack

import concourse.mybir as mybir
from concourse.masks import make_identity

V, N = 4, 512
P = 128
J = 4

FLOPS = V * 2 * 2 * N * N * N
BYTES = 2 * V * N * N * 2 + V * N * N * 4 + P * V * N * J + 16 * V * N

F32 = mybir.dt.float32
BF16 = mybir.dt.bfloat16
U32 = mybir.dt.uint32
I32 = mybir.dt.int32
U8 = mybir.dt.uint8
FP8X4 = mybir.dt.float8_e4m3fn_x4
ADD, SUBTRACT, MULT = mybir.AluOpType.add, mybir.AluOpType.subtract, mybir.AluOpType.mult
COPY, ABS = mybir.ActivationFunctionType.Copy, mybir.ActivationFunctionType.Abs

THIRD = 1.0 / 3.0
EPS = 1e-6
LAST = V - 1

TENSOR = [
    ("warm_up", 0, 9), ("sum", 1, 2), ("turn", 0, 2), ("sum", 2, 2), ("sum", 1, 1), ("sum", 3, 1), ("sum", 2, 1),
    ("sum", 3, 1), ("sum", 1, 1), ("sum", 3, 1), ("sum", 2, 1), ("sum", 3, 1), ("turn", 1, 2), ("mm1", 0, 4),
    ("mm2", 0, 4), ("turn", 2, 2), ("mm1", 1, 4), ("mm2", 1, 2), ("mm1", 2, 2), ("mm2", 1, 1),
    ("flip", 0, 1), ("mm2", 1, 1), ("mm1", 2, 2), ("turn", 3, 1), ("flip", 0, 1), ("turn", 3, 1), ("mm2", 2, 3),
    ("mm1", 3, 1), ("mm2", 2, 1), ("mm1", 3, 3), ("flip", 0, 2), ("flip", 1, 1), ("mm2", 3, 3), ("flip", 1, 1),
    ("mm2", 3, 1), ("flip", 1, 2), ("flip", 2, 4), ("flip", 3, 4),
]
SCALAR = [
    ("turn_out", 0, 2), ("mean0", 0, 4), ("turn_out", 1, 2), ("t_out", 0, 4), ("magnitude", 0, 4), ("turn_out", 2, 2),
    ("scale", 0, 4), ("t_out", 1, 4), ("magnitude", 1, 2), ("t_out", 2, 2), ("magnitude", 1, 2), ("t_out", 2, 2), ("scale", 1, 2),
    ("turn_out", 3, 2), ("magnitude", 2, 4), ("t_out", 3, 2), ("scale", 2, 3), ("magnitude", 3, 4), ("cast", 0, 1),
    ("scale", 3, 4), ("cast", 1, 1), ("cast", 2, 1), ("cast", 1, 1), ("cast", 3, 1), ("cast", 2, 1),
]
VECTOR = [
    ("quant_s", 0, 1), ("total", 0, 3), ("quant_m", 0, 1), ("others", 2, 1), ("others", 1, 1), ("quant_t", 0, 1),
    ("total", 0, 1), ("quant_t", 0, 1), ("others", 3, 1), ("others", 1, 1), ("divisor", 0, 1), ("mean", 1, 1),
    ("gain", 0, 1), ("mean", 1, 1), ("quant_s", 1, 1), ("quant_m", 1, 1), ("others", 2, 1), ("mean", 2, 2),
    ("quant_t", 1, 1), ("quant_m", 2, 1), ("quant_s", 2, 1), ("quant_t", 1, 1), ("others", 3, 1), ("join", 0, 1),
    ("mean", 3, 1), ("divisor", 1, 1), ("quant_t", 2, 1), ("gain", 1, 1), ("mean", 3, 1), ("scale", 1, 2),
    ("quant_t", 2, 1), ("quant_m", 3, 1), ("quant_s", 3, 1), ("join", 0, 1), ("t_out", 3, 2), ("divisor", 2, 1),
    ("gain", 2, 1), ("quant_t", 3, 1), ("scale", 2, 1), ("quant_t", 3, 1), ("join", 0, 2), ("join", 1, 1),
    ("cast", 0, 1), ("join", 1, 1), ("divisor", 3, 1), ("join", 1, 1), ("gain", 3, 1), ("join", 1, 1), ("join", 2, 4),
    ("quant_out", 0, 2), ("join", 3, 1), ("quant_out", 1, 1), ("join", 3, 2), ("quant_out", 2, 1), ("join", 3, 5),
    ("quant_out", 1, 1), ("cast", 3, 1, 1), ("quant_out", 3, 2), ("quant_out", 2, 1),
]


def expand(runs, counts):
    steps = []
    for stage, v, length, *first in runs:
        if not first:
            first = [counts.get((stage, v), 0)]
            counts[stage, v] = first[0] + length
        steps.extend((stage, v, first[0] + k) for k in range(length))
    return steps


def reads(stage, v, i):
    halves, quarters = range(2), range(J)
    two = (2 * i, 2 * i + 1)
    if stage == "turn_out":
        return [("turn", v, i)]
    if stage == "quant_s":
        return [("turn_out", v, k) for k in halves]
    if stage == "sum" and v > 1:
        return [("sum", v - 1, i)]
    if stage == "mean0" or stage == "total":
        return [("sum", LAST, i)]
    if stage == "others":
        return [("total", 0, k) for k in two]
    if stage == "mean":
        return [("others", v, i)]
    if stage == "quant_m":
        return [("mean0", 0, k) for k in quarters] if v == 0 else [("mean", v, k) for k in halves]
    if stage == "mm1":
        return [("quant_m", v, 0), ("quant_s", v, 0)]
    if stage == "t_out":
        return [("mm1", v, i)]
    if stage == "quant_t":
        return [("t_out", v, k) for k in two]
    if stage == "mm2":
        return [("quant_t", v, i // 2)]
    if stage == "magnitude":
        return [("mm2", v, i)]
    if stage == "divisor":
        return [("magnitude", v, k) for k in quarters]
    if stage == "gain":
        return [("divisor", v, 0)]
    if stage == "scale":
        return [("gain", v, 0)]
    if stage == "flip":
        return [("scale", v, k) for k in quarters]
    if stage == "join":
        return [("flip", v, i % J)]
    if stage == "cast":
        return [("join", v, k + (J * i if v == LAST else 0)) for k in quarters]
    if stage == "quant_out":
        return [("cast", v, i)]
    return []


def tile_signedsimilaritynetworkcrossdiffusion_x1_kernel(tc, s, p, out_0, out_1, out_2):
    nc = tc.nc
    out_words = out_1[0].rearrange("b m n -> b (m n)").bitcast(I32)
    out_scales = out_2[0].bitcast(I32)

    with ExitStack() as ctx:
        pool = ctx.enter_context(tc.tile_pool(name="pool", bufs=1))
        psum = ctx.enter_context(tc.psum_pool(name="psum", bufs=4))
        ctx.enter_context(tc.manual_schedule())
        made = {}

        def sbuf(name, v, shape, dt, bufs):
            if (name, v) not in made:
                made[name, v] = pool.tile(shape, dt, name=name, tag=name, bufs=bufs, align_bytes=64)
            return made[name, v]

        def bank(name, v, i, *shape):
            if (name, v, i) not in made:
                tag = "read_again" if name in ("sum", "q") else "read_once"
                made[name, v, i] = psum.tile([P] + list(shape), F32, name=name, tag=tag, bufs=4)
            return made[name, v, i]

        def s_rows(v):
            return sbuf("s_rows" + str(v), v, [P, J, N], BF16, 1)

        def p_rows(v):
            return sbuf("p_rows" + str(v), v, [P, J, N], BF16, 1)

        def quantised(name, v):
            return sbuf(name + "_codes", v, [P, N], U32, 4), sbuf(name + "_scales", v, [P, N], U8, 4)

        def s_turned(v):
            return sbuf("s_turned", v, [P, N, J], BF16, 3)

        def total():
            return sbuf("total", 0, [P, J, P, J], F32, 1)

        def others(v):
            return sbuf("others", v, [P, J, P, J], F32, 3)

        def mean(v):
            return sbuf("mean", v, [P, J, P, J], BF16, 3)

        def t_turned(v):
            return sbuf("t_turned", v, [P, N, J], BF16, 3)

        def column(name, v):
            return sbuf(name, v, [P, J], F32, 4)

        def scaled(v):
            return sbuf("scaled", v, [P, J, N], F32, 3)

        def result(v):
            return sbuf("result", v, [P, J, N], F32, 4)

        def rounded(v):
            return sbuf("rounded", v, [P, N, J], BF16, 3)

        def result_codes(v):
            return sbuf("result_codes", v, [P, N], U32, 4)

        def result_scales():
            return sbuf("result_scales", 0, [P, V * N], U8, 1)

        def chunk(i, width=P):
            return slice(i * width, (i + 1) * width)

        def copy(engine, out, in_):
            if engine == "scalar":
                nc.scalar.copy(out, in_)
            else:
                nc.vector.tensor_copy(out=out, in_=in_)

        def times(engine, out, in_, factor):
            if engine == "scalar":
                nc.scalar.activation(out=out, in_=in_, func=COPY, scale=factor)
            else:
                nc.vector.tensor_scalar(out=out, in0=in_, scalar1=factor, scalar2=None, op0=MULT)

        def quantize(code_words, scale_bytes, values):
            nc.vector.quantize_mx(out=code_words.bitcast(FP8X4), scales=scale_bytes, in_=values)

        def product(out, left, left_columns, right, right_columns):
            nc.tensor.matmul_mx(
                out=out,
                lhsT=left[0][:, left_columns].bitcast(FP8X4),
                lhsT_scale=left[1][:, left_columns],
                rhs=right[0][:, right_columns].bitcast(FP8X4),
                rhs_scale=right[1][:, right_columns],
                start=True,
                stop=True,
            )


        def warm_up(v, i, engine):
            flat = bank("sum", 0, 0, J, P)[:].rearrange("b k a -> b (k a)")
            product(flat[:, chunk(0, 2 * P)], zeros, chunk(0), zeros, chunk(0, 2 * P))

        def turn(v, i, engine):
            words = s_rows(v)[:].bitcast(F32)
            for n in range(2):
                for w in range(2):
                    nc.tensor.transpose(bank("s", v, i, 2, 2, P)[:, n, w, :], words[:, 2 * i + n, w::2], identity[:])

        def turn_out(v, i, engine):
            out = s_turned(v)[:, chunk(i, 2 * P), :].rearrange("b c k -> b (c k)").bitcast(F32)
            copy(engine, out.rearrange("b (n a w) -> b n a w", n=2, w=2), bank("s", v, i)[:].rearrange("b n w a -> b n a w"))

        def quant_s(v, i, engine):
            codes, scales = quantised("s", v)
            quantize(codes[:], scales[:], s_turned(v)[:].rearrange("b c k -> b (c k)"))

        def sum_p(v, i, engine):
            columns = p_rows(v)[:, :, i::J]
            nc.tensor.matmul(bank("sum", 0, i, J, P)[:], lhsT=identity_bf[:], rhs=columns, start=(v == 1), stop=(v == LAST))

        def mean_0(v, i, engine):
            times(engine, mean(0)[:, i], bank("sum", 0, i)[:].rearrange("b k a -> b a k"), THIRD)

        def add_p0(v, i, engine):
            nc.vector.tensor_tensor(
                out=total()[:, i],
                in0=bank("sum", 0, i)[:].rearrange("b k a -> b a k"),
                in1=p_rows(0)[:, :, i::J].rearrange("b k a -> b a k"),
                op=ADD,
            )

        def subtract_own(v, i, engine):
            own = p_rows(v)[:].rearrange("b k (a n) -> b n a k", n=J)
            two = chunk(i, 2)
            nc.vector.tensor_tensor(out=others(v)[:, two], in0=total()[:, two], in1=own[:, two], op=SUBTRACT)

        def take_third(v, i, engine):
            flat, two = "b n a k -> b (n a k)", chunk(i, 2)
            times(engine, mean(v)[:, two].rearrange(flat), others(v)[:, two].rearrange(flat), THIRD)

        def quant_m(v, i, engine):
            codes, scales = quantised("m", v)
            quantize(codes[:], scales[:], mean(v)[:].rearrange("b n a k -> b (n a k)"))

        def mm1(v, i, engine):
            for n in range(J):
                product(bank("t", v, i, J, P)[:, n, :], quantised("m", v), chunk(n), quantised("s", v), chunk(i))

        def t_out(v, i, engine):
            copy(engine, t_turned(v)[:, chunk(i), :], bank("t", v, i)[:].rearrange("b n a -> b a n"))

        def quant_t(v, i, engine):
            (codes, scales), half = quantised("t", v), chunk(i, 2 * P)
            quantize(codes[:, half], scales[:, half], t_turned(v)[:, half, :].rearrange("b c k -> b (c k)"))

        def mm2(v, i, engine):
            product(bank("q", v, i, N)[:], quantised("t", v), chunk(i), quantised("s", v), chunk(0, N))

        def magnitude(v, i, engine):
            written = sbuf("magnitudes", (v, i), [P, N], F32, 2)
            sums = column("two_d", v)[:, i : i + 1]
            nc.scalar.activation(out=written[:], in_=bank("q", v, i)[:], func=ABS, scale=2.0 / N, accum_out=sums)

        def divisor(v, i, engine):
            out = column("divisor", v)
            nc.vector.tensor_scalar(out=out[:], in0=column("two_d", v)[:], scalar1=2 * EPS, scalar2=None, op0=ADD)

        def gain(v, i, engine):
            nc.vector.reciprocal(out=column("gain", v)[:], in_=column("divisor", v)[:])

        def scale(v, i, engine):
            times(engine, scaled(v)[:, i, :], bank("q", v, i)[:], column("gain", v)[:, i : i + 1])

        def flip(v, i, engine):
            for n in range(J):
                nc.tensor.transpose(bank("flip", v, i, J, P)[:, n, :], scaled(v)[:, n, chunk(i)], identity[:])

        def join(v, i, engine):
            parts = 2 if v == LAST else 1
            n, part = i % J, i // J
            a, columns = chunk(part, P // parts), chunk(part, N // parts)
            nc.vector.tensor_tensor(
                out=result(v)[:, n, columns].rearrange("b (a k) -> b a k", k=J),
                in0=bank("flip", v, n)[:, :, a].rearrange("b k a -> b a k"),
                in1=scaled(v)[:, n, :].rearrange("b (k a) -> b a k", k=J)[:, a, :],
                op=ADD,
            )
            if n == J - 1:
                rows = out_0[v].rearrange("(b n) l -> b n l", n=J)
                nc.sync.dma_start(out=rows[:, :, columns], in_=result(v)[:, :, columns])

        def cast(v, i, engine):
            half = chunk(i, N // 2)
            copy(engine, rounded(v)[:, half, :], result(v)[:, :, half].rearrange("b n l -> b l n"))

        def quant_out(v, i, engine):
            half, place = chunk(i, N // 2), chunk(2 * v + i, N // 2)
            quantize(result_codes(v)[:, half], result_scales()[:, place], rounded(v)[:, half, :].rearrange("b l n -> b (l n)"))
            nc.sync.dma_start(out=out_words[:, place], in_=result_codes(v)[:, half].bitcast(I32))

        do = {
            "warm_up": warm_up,
            "turn": turn,
            "turn_out": turn_out,
            "quant_s": quant_s,
            "sum": sum_p,
            "mean0": mean_0,
            "total": add_p0,
            "others": subtract_own,
            "mean": take_third,
            "quant_m": quant_m,
            "mm1": mm1,
            "t_out": t_out,
            "quant_t": quant_t,
            "mm2": mm2,
            "magnitude": magnitude,
            "divisor": divisor,
            "gain": gain,
            "scale": scale,
            "flip": flip,
            "join": join,
            "cast": cast,
            "quant_out": quant_out,
        }

        def load(tile, source, first, count):
            neighbours = slice(first, first + count)
            nc.sync.dma_start(out=tile[:, neighbours, :], in_=source.rearrange("(b n) k -> b n k", n=J)[:, neighbours, :])

        load(p_rows(1), p[1], 0, J)
        for first in (0, 2):
            load(s_rows(0), s[0], first, 2)
        for v in (2, 3, 0):
            load(p_rows(v), p[v], 0, J)
        for v in range(1, V):
            load(s_rows(v), s[v], 0, J)

        identity = sbuf("identity", 0, [P, P], F32, 1)
        identity_bf = sbuf("identity_bf", 0, [P, P], BF16, 1)
        make_identity(nc, identity_bf[:])
        make_identity(nc, identity[:])

        zero_rows = sbuf("zero_rows", 0, [P, 2 * P * J], BF16, 1)
        zeros = sbuf("zero_codes", 0, [P, 2 * P], U32, 1), sbuf("zero_scales", 0, [P, 2 * P], U8, 1)
        nc.vector.memset(zero_rows[:], 0.0)
        quantize(zeros[0][:], zeros[1][:], zero_rows[:])

        counts = {}
        queues = [("vector", expand(VECTOR, counts)), ("scalar", expand(SCALAR, counts)), ("tensor", expand(TENSOR, counts))]
        written = set()
        while any(steps for engine, steps in queues):
            for engine, steps in queues:
                while steps and all(step in written for step in reads(*steps[0])):
                    stage, v, i = steps[0]
                    do[stage](v, i, engine)
                    written.add(steps[0])
                    steps.remove(steps[0])

        for Q in range(4):
            in_ = result_scales()[32 * Q : 32 * Q + 4, :].bitcast(I32)
            nc.sync.dma_start(out=out_scales[4 * Q : 4 * Q + 4, :], in_=in_)
